import numpy as np
import ml_dtypes


def mxq(x, axis, fmt="e4m3"):
    dtype, down = {"e4m3": (ml_dtypes.float8_e4m3fn, 7), "e5m2": (ml_dtypes.float8_e5m2, 14)}[fmt]
    v = np.moveaxis(np.asarray(x, np.float32).astype(ml_dtypes.bfloat16).astype(np.float64), axis, -1)
    blocks = v.reshape(v.shape[:-1] + (-1, 32))
    amax = np.abs(blocks).max(-1, keepdims=True)
    byte = np.maximum(np.where(amax > 0, np.frexp(amax)[1] - 1 + 127, 0) - down, 1)
    scale = np.exp2(byte - 127.0)
    codes = (blocks / scale).astype(np.float32).astype(dtype).astype(np.float64)
    return np.moveaxis((codes * scale).reshape(v.shape), -1, axis)


WIDE = False


def mx_kscale(k):
    if not WIDE:
        return np.ones(k)
    levels = np.array([10, -10, 5, -5, 0])
    if k % 512:
        return np.exp2(np.random.permutation(np.resize(levels, k // 32))).repeat(32)
    a = np.empty((k // 512, 16))
    for p in range(k // 512):
        a[p, :8] = np.random.permutation(np.resize(levels, 8))
        for g in range(8):
            far = levels[np.abs(levels - a[p, g]) >= 10]
            a[p, g + 8] = far[np.random.randint(len(far))]
    return np.exp2(a.ravel()).repeat(32)


def f64(x):
    return np.asarray(x).astype(np.float64)


def striped(idx):
    return np.tile(np.asarray(idx).reshape(-1, 16).T, (8, 1)).astype(np.uint16)


def unstriped(offs):
    return offs[:16].T.reshape(-1).astype(np.int64)


E2M1 = np.array([0.0, 0.5, 1.0, 1.5, 2.0, 3.0, 4.0, 6.0, -0.0, -0.5, -1.0, -1.5, -2.0, -3.0, -4.0, -6.0])


def pack_weight(w, fmt):
    k, n = w.shape
    w = f64(np.asarray(w, np.float32).astype(ml_dtypes.bfloat16)).reshape(k // 32, 32, n)
    amax = np.abs(w).max(1)
    if fmt == "e4m3":
        byte = np.frexp(amax)[1] - 1 + 127 - 7
    else:
        mant, ex = np.frexp(amax / 6.0)
        byte = np.where(mant > 0.5, ex, ex - 1) + 127
    byte = np.clip(np.where(amax > 0, byte, 1), 1, 254)
    scaled = (w * np.exp2(127.0 - byte)[:, None, :]).reshape(k, n).astype(np.float32)
    by_word = np.ascontiguousarray(scaled.reshape(k // 512, 128, 4, n).transpose(0, 1, 3, 2))
    if fmt == "e4m3":
        words = by_word.astype(ml_dtypes.float8_e4m3fn).view(np.uint8)
    else:
        c = by_word.astype(ml_dtypes.float4_e2m1fn).view(np.uint8) & 0xF
        words = (c[..., 0::2] | (c[..., 1::2] << 4)).reshape(k // 512, 128, 2 * n)
    return np.ascontiguousarray(words), np.ascontiguousarray(byte.astype(np.uint8).reshape(k // 512, 16, n))


def unpack_weight(words, scales, fmt):
    g, _, n = scales.shape
    words = np.ascontiguousarray(words).reshape(g, 128, n, -1)
    if fmt == "e4m3":
        vals = words.view(ml_dtypes.float8_e4m3fn).astype(np.float64)
    else:
        nib = np.empty((g, 128, n, 4), np.uint8)
        nib[..., 0::2] = words & 0xF
        nib[..., 1::2] = words >> 4
        vals = E2M1[nib]
    vals = vals * np.repeat(np.exp2(scales.astype(np.float64) - 127.0), 8, axis=1)[..., None]
    return vals.transpose(0, 1, 3, 2).reshape(g * 512, n)


def bf(x):
    return np.asarray(x, np.float32).astype(ml_dtypes.bfloat16)


def planes(Y):
    r, m = Y.shape
    b = f64(bf(Y)).reshape(r // 32, 32, m)
    amax = np.abs(b).max(1)
    byte = np.clip(np.where(amax > 0, np.frexp(amax)[1] - 1 + 127 - 7, 1), 1, 254)
    codes = (b * np.exp2(127.0 - byte)[:, None, :]).reshape(r, m).astype(np.float32).astype(ml_dtypes.float8_e4m3fn).view(np.uint8)
    words = codes.reshape(r // 512, 128, 4, m).transpose(0, 1, 3, 2)
    return np.ascontiguousarray(words), np.ascontiguousarray(byte.astype(np.uint8).reshape(r // 512, 16, m))


K, T, J, N = 1024, 2048, 512, 512


def setup_inputs():
    n = np.random.standard_normal
    idx = np.random.permutation(T)[:J]
    fk = mx_kscale(K)
    wap = pack_weight(n((K, N)) * 1 / np.sqrt(K) * fk[:, None], "e2m1")
    wbp = pack_weight(n((K, N)) * 1 / np.sqrt(K) * fk[:, None], "e4m3")
    return {
        "xt": (n((K, T)) / fk[:, None]).astype(np.float32),
        "wa_words": wap[0],
        "wa_scales": wap[1],
        "wb_words": wbp[0],
        "wb_scales": wbp[1],
        "ga": (np.random.uniform(0.4, 1.2, (1, J))).astype(np.float32),
        "offs": striped(idx),
    }


def reference(xt, wa_words, wa_scales, wb_words, wb_scales, ga, offs):
    idx = unstriped(offs)
    wau = unpack_weight(wa_words, wa_scales, "e2m1")
    wbu = unpack_weight(wb_words, wb_scales, "e4m3")
    xtidxq = mxq(f64(xt)[:, idx], 0, "e4m3")
    a = wau.T @ xtidxq
    b = wbu.T @ xtidxq
    ea = np.exp(0.5 * a)
    eb = np.exp(0.5 * b)
    y = f64(ga) * (ea * a + eb * b) / (ea + eb)
    words, scales = planes(y)
    return y, words, scales

@@ -1,0 +1,195 @@
+from contextlib import ExitStack
+
+import concourse.mybir as mybir
+from concourse.masks import make_identity
+
+K, T, J, N = 1024, 2048, 512, 512
+FLOPS = 2 * 2 * K * N * J
+
+F32 = mybir.dt.float32
+BF16 = mybir.dt.bfloat16
+I32 = mybir.dt.int32
+U32 = mybir.dt.uint32
+U16 = mybir.dt.uint16
+U8 = mybir.dt.uint8
+FP8X4 = mybir.dt.float8_e4m3fn_x4
+FP4X4 = mybir.dt.float4_e2m1fn_x4
+ALU = mybir.AluOpType
+ACT = mybir.ActivationFunctionType
+
+P = 128
+PACK = 4
+PASSES = K // (P * PACK)
+CHUNK = 128
+CHUNKS = J // CHUNK
+HALF = J // 2
+B_ROW = 4
+
+
+def deal_columns(nc, dealt, raw, run):
+    nc.vector.tensor_copy(
+        out=dealt.rearrange("p z (t c i) -> p z c t i", t=PACK, i=run),
+        in_=raw.rearrange("p z (c i t) -> p z c t i", t=PACK, i=run),
+    )
+
+
+def tile_moe_soft_larger_of_two_experts_pl_kernel(
+    tc, xt, wa_words, wa_scales, wb_words, wb_scales, ga, offs, out_0, out_1, out_2
+):
+    nc = tc.nc
+    x_rows = xt.rearrange("(z p t) c -> z t p c", p=P, t=PACK)
+    y_rows = out_0.rearrange("(p t) j -> p t j", t=PACK)
+    y_words = out_1[0].rearrange("p j t -> p (j t)").bitcast(I32)
+    y_scales = out_2[0].bitcast(I32)
+
+    with ExitStack() as ctx:
+        keep = ctx.enter_context(tc.tile_pool(name="keep", bufs=1))
+        stream = ctx.enter_context(tc.tile_pool(name="stream", bufs=4))
+        work = ctx.enter_context(tc.tile_pool(name="work", bufs=4))
+        psum = ctx.enter_context(tc.psum_pool(name="psum", bufs=1))
+
+        offsets = keep.tile([P, J // 16], U16, name="offsets")
+        nc.sync.dma_start(offsets[:], offs)
+
+        raw_scales = keep.tile([P, PASSES, N], U8, name="raw_scales", align_bytes=64)
+        nc.gpsimd.memset(raw_scales[:].bitcast(I32), 0)
+        ident = keep.tile([P, P], F32, name="ident")
+        make_identity(nc, ident[:])
+        warm = keep.tile([P, 1], F32, name="warm")
+        nc.scalar.activation(warm[:], ident[:, 0:1], ACT.Silu)
+
+        def load_x(z, t):
+            rows = stream.tile([P, T], F32, name="x_rows", tag="x_rows")
+            nc.sync.dma_start(rows[:], x_rows[z, t])
+            return rows
+
+        x_tiles = {(0, 0): load_x(0, 0)}
+
+        raw_a = keep.tile([P, PASSES, 2 * N], U8, name="raw_a", align_bytes=64)
+        nc.sync.dma_start(raw_a[:].bitcast(I32), wa_words.rearrange("z p c -> p z c").bitcast(I32))
+        raw_b = keep.tile([P, PASSES, N], I32, name="raw_b", align_bytes=64)
+        nc.sync.dma_start(raw_b[:], wb_words.rearrange("z p n t -> p z (n t)").bitcast(I32))
+        for first_row, scales in ((0, wa_scales), (B_ROW, wb_scales)):
+            for r in range(4):
+                nc.scalar.dma_start(
+                    raw_scales[first_row + r : P : 32].bitcast(I32),
+                    scales[:, r:16:4, :].rearrange("z q c -> q z c").bitcast(I32),
+                )
+        gate_cols = keep.tile([P, CHUNKS], F32, name="gate_cols")
+        nc.scalar.dma_start(gate_cols[:], ga.rearrange("o (p c) -> (o p) c", c=CHUNKS))
+
+        acc_a = [psum.tile([P, PACK, CHUNK], F32, name=f"acc_a{c}") for c in range(CHUNKS)]
+        acc_b = [psum.tile([P, PACK, CHUNK], F32, name=f"acc_b{c}") for c in range(CHUNKS)]
+
+        gate = keep.tile([P, J], F32, name="gate")
+        for c in range(CHUNKS):
+            nc.tensor.transpose(acc_a[-1][:, c, :], gate_cols[:, c : c + 1].to_broadcast([P, P]), ident[:])
+        nc.scalar.copy(gate[:].rearrange("q (p c) -> q p c", c=CHUNKS), acc_a[-1][:].rearrange("q c p -> q p c"))
+
+        a_words = keep.tile([P, PASSES, 2 * N], U8, name="a_words", align_bytes=64)
+        b_words = keep.tile([P, PASSES, N], I32, name="b_words", align_bytes=64)
+        w_scales = keep.tile([P, PASSES, N], U8, name="w_scales", align_bytes=64)
+
+        x_bf = [keep.tile([P, J, PACK], BF16, name=f"x_bf{z}", align_bytes=64) for z in range(PASSES)]
+        x_codes = [keep.tile([P, J], U32, name=f"x_codes{z}", align_bytes=64) for z in range(PASSES)]
+        x_scales = [keep.tile([P, J], U8, name=f"x_scales{z}", align_bytes=64) for z in range(PASSES)]
+
+        def quantise_x(z, j0, j1):
+            nc.vector.quantize_mx(
+                out=x_codes[z][:, j0:j1].bitcast(FP8X4),
+                scales=x_scales[z][:, j0:j1],
+                in_=x_bf[z][:, j0:j1, :].rearrange("p j t -> p (j t)"),
+            )
+
+        def multiply(z, c):
+            cols = slice(c * CHUNK, (c + 1) * CHUNK)
+            for t in range(PACK):
+                nc.tensor.matmul_mx(
+                    out=acc_b[c][:, t, :],
+                    lhsT=b_words[:, z, t * P : (t + 1) * P].bitcast(FP8X4),
+                    lhsT_scale=w_scales[B_ROW:P, z, t * P : (t + 1) * P],
+                    rhs=x_codes[z][:, cols].bitcast(FP8X4),
+                    rhs_scale=x_scales[z][:, cols],
+                    start=(z == 0 and t == 0),
+                    stop=(z == PASSES - 1 and t == PACK - 1),
+                )
+            for t in range(PACK):
+                nc.tensor.matmul_mx(
+                    out=acc_a[c][:, t, :],
+                    lhsT=a_words[:, z, 2 * t * P : 2 * (t + 1) * P].bitcast(FP4X4),
+                    lhsT_scale=w_scales[:, z, t * P : (t + 1) * P],
+                    rhs=x_codes[z][:, cols].bitcast(FP8X4),
+                    rhs_scale=x_scales[z][:, cols],
+                    start=(z == 0 and t == 0),
+                    stop=(z == PASSES - 1 and t == PACK - 1),
+                )
+
+        picked = keep.tile([P, PACK, J], F32, name="picked")
+        for t in range(PACK):
+            if t + 1 < PACK:
+                x_tiles[(0, t + 1)] = load_x(0, t + 1)
+            nc.vector.tensor_copy(picked[:, t, :], x_tiles[(0, t)][:].indirect(offsets[:]))
+            if t == 0:
+                deal_columns(nc, a_words[:].bitcast(U16), raw_a[:].bitcast(U16), 8)
+            if t == 1:
+                deal_columns(nc, b_words[:], raw_b[:], 4)
+            if t == 2:
+                deal_columns(nc, w_scales[:], raw_scales[:], 16)
+        nc.scalar.copy(
+            x_bf[0][:].rearrange("p (c i) t -> p c t i", i=4),
+            picked[:].rearrange("p t (c i) -> p c t i", i=4),
+        )
+
+        for t in range(PACK - 1):
+            rows = load_x(1, t)
+            nc.vector.tensor_copy(x_bf[1][:, :, t], rows[:].indirect(offsets[:]))
+            if t == 0:
+                quantise_x(0, 0, J)
+                for c in range(CHUNKS):
+                    multiply(0, c)
+        rows = load_x(1, PACK - 1)
+        for h in range(2):
+            nc.vector.tensor_copy(
+                x_bf[1][:, h * HALF : (h + 1) * HALF, PACK - 1],
+                rows[:].indirect(offsets[:, h * HALF // 16 : (h + 1) * HALF // 16]),
+            )
+            quantise_x(1, h * HALF, (h + 1) * HALF)
+            for c in range(h * CHUNKS // 2, (h + 1) * CHUNKS // 2):
+                multiply(1, c)
+
+        y_codes = keep.tile([P, J], U32, name="y_codes", align_bytes=64)
+        y_plane = keep.tile([P, J], U8, name="y_plane", align_bytes=64)
+        for c in range(CHUNKS):
+            cols = slice(c * CHUNK, (c + 1) * CHUNK)
+            b_sb = work.tile([P, PACK, CHUNK], F32, name="b_sb")
+            nc.scalar.copy(b_sb[:], acc_b[c][:])
+            diff = work.tile([P, PACK, CHUNK], F32, name="diff")
+            nc.vector.tensor_tensor(diff[:], acc_a[c][:], b_sb[:], ALU.subtract)
+            soft = work.tile([P, PACK, CHUNK], F32, name="soft")
+            nc.scalar.activation(soft[:], diff[:], ACT.Silu, scale=0.5)
+            mix = work.tile([P, PACK, CHUNK], F32, name="mix")
+            nc.vector.scalar_tensor_tensor(
+                mix[:].rearrange("p t j -> p (t j)"),
+                soft[:].rearrange("p t j -> p (t j)"),
+                2.0,
+                acc_b[c][:].rearrange("p t j -> p (t j)"),
+                ALU.mult,
+                ALU.add,
+            )
+            y = work.tile([P, PACK, CHUNK], F32, name="y")
+            nc.vector.tensor_tensor(y[:], mix[:], gate[:, cols].unsqueeze(1).to_broadcast([P, PACK, CHUNK]), ALU.mult)
+            nc.sync.dma_start(y_rows[:, :, cols], y[:])
+            y_bf = work.tile([P, CHUNK, PACK], BF16, name="y_bf", align_bytes=64)
+            nc.scalar.copy(
+                y_bf[:].rearrange("p (c i) t -> p c t i", i=4),
+                y[:].rearrange("p t (c i) -> p c t i", i=4),
+            )
+            nc.vector.quantize_mx(
+                out=y_codes[:, cols].bitcast(FP8X4),
+                scales=y_plane[:, cols],
+                in_=y_bf[:].rearrange("p j t -> p (j t)"),
+            )
+            nc.sync.dma_start(y_words[:, cols], y_codes[:, cols].bitcast(I32))
+        for r in range(4):
+            queue = nc.sync if r % 2 == 0 else nc.scalar
+            queue.dma_start(y_scales[r:16:4, :], y_plane[r:P:32, :].bitcast(I32))

@@ -44,7 +44,6 @@ def tile_moe_soft_larger_of_two_experts_pl_kernel(
 
     with ExitStack() as ctx:
         keep = ctx.enter_context(tc.tile_pool(name="keep", bufs=1))
-        stream = ctx.enter_context(tc.tile_pool(name="stream", bufs=4))
         work = ctx.enter_context(tc.tile_pool(name="work", bufs=4))
         psum = ctx.enter_context(tc.psum_pool(name="psum", bufs=1))
 
@@ -59,7 +58,7 @@ def tile_moe_soft_larger_of_two_experts_pl_kernel(
         nc.scalar.activation(warm[:], ident[:, 0:1], ACT.Silu)
 
         def load_x(z, t):
-            rows = stream.tile([P, T], F32, name="x_rows", tag="x_rows")
+            rows = keep.tile([P, T], F32, name=f"x_rows{z}{t}", tag=f"x_rows{t}", align_bytes=64)
             nc.sync.dma_start(rows[:], x_rows[z, t])
             return rows
 
@@ -91,25 +90,31 @@ def tile_moe_soft_larger_of_two_experts_pl_kernel(
         w_scales = keep.tile([P, PASSES, N], U8, name="w_scales", align_bytes=64)
 
         x_bf = [keep.tile([P, J, PACK], BF16, name=f"x_bf{z}", align_bytes=64) for z in range(PASSES)]
-        x_codes = [keep.tile([P, J], U32, name=f"x_codes{z}", align_bytes=64) for z in range(PASSES)]
-        x_scales = [keep.tile([P, J], U8, name=f"x_scales{z}", align_bytes=64) for z in range(PASSES)]
+        x_codes = {}
+        x_scales = {}
 
-        def quantise_x(z, j0, j1):
+        def quantise_x(z, h):
+            tag = f"x_rows{PACK - 2}" if (z, h) == (0, 1) else f"x_codes{z}{h}"
+            x_codes[z, h] = keep.tile([P, HALF], U32, name=f"x_codes{z}{h}", tag=tag, align_bytes=64)
+            x_scales[z, h] = keep.tile([P, HALF], U8, name=f"x_scales{z}{h}", align_bytes=64)
             nc.vector.quantize_mx(
-                out=x_codes[z][:, j0:j1].bitcast(FP8X4),
-                scales=x_scales[z][:, j0:j1],
-                in_=x_bf[z][:, j0:j1, :].rearrange("p j t -> p (j t)"),
+                out=x_codes[z, h][:].bitcast(FP8X4),
+                scales=x_scales[z, h][:],
+                in_=x_bf[z][:, h * HALF : (h + 1) * HALF, :].rearrange("p j t -> p (j t)"),
             )
+            for c in range(2 * h, 2 * h + 2):
+                multiply(z, c)
 
         def multiply(z, c):
-            cols = slice(c * CHUNK, (c + 1) * CHUNK)
+            h = c // 2
+            cols = slice(c % 2 * CHUNK, (c % 2 + 1) * CHUNK)
             for t in range(PACK):
                 nc.tensor.matmul_mx(
                     out=acc_b[c][:, t, :],
                     lhsT=b_words[:, z, t * P : (t + 1) * P].bitcast(FP8X4),
                     lhsT_scale=w_scales[B_ROW:P, z, t * P : (t + 1) * P],
-                    rhs=x_codes[z][:, cols].bitcast(FP8X4),
-                    rhs_scale=x_scales[z][:, cols],
+                    rhs=x_codes[z, h][:, cols].bitcast(FP8X4),
+                    rhs_scale=x_scales[z, h][:, cols],
                     start=(z == 0 and t == 0),
                     stop=(z == PASSES - 1 and t == PACK - 1),
                 )
@@ -118,8 +123,8 @@ def tile_moe_soft_larger_of_two_experts_pl_kernel(
                     out=acc_a[c][:, t, :],
                     lhsT=a_words[:, z, 2 * t * P : 2 * (t + 1) * P].bitcast(FP4X4),
                     lhsT_scale=w_scales[:, z, t * P : (t + 1) * P],
-                    rhs=x_codes[z][:, cols].bitcast(FP8X4),
-                    rhs_scale=x_scales[z][:, cols],
+                    rhs=x_codes[z, h][:, cols].bitcast(FP8X4),
+                    rhs_scale=x_scales[z, h][:, cols],
                     start=(z == 0 and t == 0),
                     stop=(z == PASSES - 1 and t == PACK - 1),
                 )
@@ -144,46 +149,80 @@ def tile_moe_soft_larger_of_two_experts_pl_kernel(
             rows = load_x(1, t)
             nc.vector.tensor_copy(x_bf[1][:, :, t], rows[:].indirect(offsets[:]))
             if t == 0:
-                quantise_x(0, 0, J)
-                for c in range(CHUNKS):
-                    multiply(0, c)
+                quantise_x(0, 0)
+        quantise_x(0, 1)
         rows = load_x(1, PACK - 1)
         for h in range(2):
             nc.vector.tensor_copy(
                 x_bf[1][:, h * HALF : (h + 1) * HALF, PACK - 1],
                 rows[:].indirect(offsets[:, h * HALF // 16 : (h + 1) * HALF // 16]),
             )
-            quantise_x(1, h * HALF, (h + 1) * HALF)
-            for c in range(h * CHUNKS // 2, (h + 1) * CHUNKS // 2):
-                multiply(1, c)
+            quantise_x(1, h)
 
         y_codes = keep.tile([P, J], U32, name="y_codes", align_bytes=64)
         y_plane = keep.tile([P, J], U8, name="y_plane", align_bytes=64)
-        for c in range(CHUNKS):
-            cols = slice(c * CHUNK, (c + 1) * CHUNK)
+        last = CHUNKS - 1
+        diff, soft, mix, y = {}, {}, {}, {}
+
+        def subtract(c):
             b_sb = work.tile([P, PACK, CHUNK], F32, name="b_sb")
             nc.scalar.copy(b_sb[:], acc_b[c][:])
-            diff = work.tile([P, PACK, CHUNK], F32, name="diff")
-            nc.vector.tensor_tensor(diff[:], acc_a[c][:], b_sb[:], ALU.subtract)
+            diff[c] = keep.tile([P, PACK, CHUNK], F32, name=f"diff{c}", tag=f"diff{c}", align_bytes=64)
+            nc.vector.tensor_tensor(diff[c][:], acc_a[c][:], b_sb[:], ALU.subtract)
+
+        def blend(c):
             soft = work.tile([P, PACK, CHUNK], F32, name="soft")
-            nc.scalar.activation(soft[:], diff[:], ACT.Silu, scale=0.5)
-            mix = work.tile([P, PACK, CHUNK], F32, name="mix")
+            nc.scalar.activation(soft[:], diff[c][:], ACT.Silu, scale=0.5)
+            mix[c] = work.tile([P, PACK, CHUNK], F32, name="mix")
             nc.vector.scalar_tensor_tensor(
-                mix[:].rearrange("p t j -> p (t j)"),
+                mix[c][:].rearrange("p t j -> p (t j)"),
                 soft[:].rearrange("p t j -> p (t j)"),
                 2.0,
                 acc_b[c][:].rearrange("p t j -> p (t j)"),
                 ALU.mult,
                 ALU.add,
             )
-            y = work.tile([P, PACK, CHUNK], F32, name="y")
-            nc.vector.tensor_tensor(y[:], mix[:], gate[:, cols].unsqueeze(1).to_broadcast([P, PACK, CHUNK]), ALU.mult)
-            nc.sync.dma_start(y_rows[:, :, cols], y[:])
-            y_bf = work.tile([P, CHUNK, PACK], BF16, name="y_bf", align_bytes=64)
-            nc.scalar.copy(
-                y_bf[:].rearrange("p (c i) t -> p c t i", i=4),
-                y[:].rearrange("p t (c i) -> p c t i", i=4),
-            )
+
+        def weigh(c):
+            cols = slice(c * CHUNK, (c + 1) * CHUNK)
+            y[c] = work.tile([P, PACK, CHUNK], F32, name="y")
+            if c < 2:
+                nc.gpsimd.tensor_tensor(
+                    y[c][:], mix[c][:], gate[:, cols].unsqueeze(1).to_broadcast([P, PACK, CHUNK]), ALU.mult
+                )
+            else:
+                quarter = CHUNK // CHUNKS
+                gate_psum = acc_a[0][:].rearrange("q r p -> q p r")[:, c * quarter : (c + 1) * quarter, :]
+                nc.vector.tensor_tensor(
+                    y[c][:].rearrange("p t (a r) -> p t a r", r=CHUNKS),
+                    mix[c][:].rearrange("p t (a r) -> p t a r", r=CHUNKS),
+                    gate_psum.unsqueeze(1).to_broadcast([P, PACK, quarter, CHUNKS]),
+                    ALU.mult,
+                )
+            nc.sync.dma_start(y_rows[:, :, cols], y[c][:])
+
+        subtract(0)
+        for r in range(CHUNKS):
+            nc.tensor.transpose(acc_a[0][:, r, :], gate_cols[:, r : r + 1].to_broadcast([P, P]), ident[:])
+        subtract(1)
+        subtract(2)
+        blend(0)
+        subtract(3)
+        for c in range(1, CHUNKS):
+            blend(c)
+        for c in range(CHUNKS):
+            weigh(c)
+        for h in range(2):
+            y_bf = keep.tile([P, HALF, PACK], BF16, name=f"y_bf{h}", tag=f"diff{last - h}", align_bytes=64)
+            for i in range(2):
+                c = 2 * h + i
+                dst = y_bf[:, i * CHUNK : (i + 1) * CHUNK, :].rearrange("p (c i) t -> p c t i", i=4)
+                src = y[c][:].rearrange("p t (c i) -> p c t i", i=4)
+                if c < last:
+                    nc.scalar.copy(dst, src)
+                else:
+                    nc.vector.tensor_copy(dst, src)
+            cols = slice(h * HALF, (h + 1) * HALF)
             nc.vector.quantize_mx(
                 out=y_codes[:, cols].bitcast(FP8X4),
                 scales=y_plane[:, cols],

@@ -90,31 +90,28 @@ def tile_moe_soft_larger_of_two_experts_pl_kernel(
         w_scales = keep.tile([P, PASSES, N], U8, name="w_scales", align_bytes=64)
 
         x_bf = [keep.tile([P, J, PACK], BF16, name=f"x_bf{z}", align_bytes=64) for z in range(PASSES)]
-        x_codes = {}
-        x_scales = {}
 
-        def quantise_x(z, h):
-            tag = f"x_rows{PACK - 2}" if (z, h) == (0, 1) else f"x_codes{z}{h}"
-            x_codes[z, h] = keep.tile([P, HALF], U32, name=f"x_codes{z}{h}", tag=tag, align_bytes=64)
-            x_scales[z, h] = keep.tile([P, HALF], U8, name=f"x_scales{z}{h}", align_bytes=64)
+        def quantise_x(z, chunks, place, tag=None):
+            width = len(chunks) * CHUNK
+            name = f"{z}{chunks[0]}"
+            codes = keep.tile([P, width], U32, name=f"x_codes{name}", tag=tag or f"x_codes{name}", align_bytes=64)
+            scales = keep.tile([P, width], U8, name=f"x_scales{name}", align_bytes=64)
             nc.vector.quantize_mx(
-                out=x_codes[z, h][:].bitcast(FP8X4),
-                scales=x_scales[z, h][:],
-                in_=x_bf[z][:, h * HALF : (h + 1) * HALF, :].rearrange("p j t -> p (j t)"),
+                out=codes[:].bitcast(FP8X4),
+                scales=scales[:],
+                in_=x_bf[z][:, place * CHUNK : place * CHUNK + width, :].rearrange("p j t -> p (j t)"),
             )
-            for c in range(2 * h, 2 * h + 2):
-                multiply(z, c)
+            for i, c in enumerate(chunks):
+                multiply(z, c, codes[:, i * CHUNK : (i + 1) * CHUNK], scales[:, i * CHUNK : (i + 1) * CHUNK])
 
-        def multiply(z, c):
-            h = c // 2
-            cols = slice(c % 2 * CHUNK, (c % 2 + 1) * CHUNK)
+        def multiply(z, c, codes, scales):
             for t in range(PACK):
                 nc.tensor.matmul_mx(
                     out=acc_b[c][:, t, :],
                     lhsT=b_words[:, z, t * P : (t + 1) * P].bitcast(FP8X4),
                     lhsT_scale=w_scales[B_ROW:P, z, t * P : (t + 1) * P],
-                    rhs=x_codes[z, h][:, cols].bitcast(FP8X4),
-                    rhs_scale=x_scales[z, h][:, cols],
+                    rhs=codes.bitcast(FP8X4),
+                    rhs_scale=scales,
                     start=(z == 0 and t == 0),
                     stop=(z == PASSES - 1 and t == PACK - 1),
                 )
@@ -123,8 +120,8 @@ def tile_moe_soft_larger_of_two_experts_pl_kernel(
                     out=acc_a[c][:, t, :],
                     lhsT=a_words[:, z, 2 * t * P : 2 * (t + 1) * P].bitcast(FP4X4),
                     lhsT_scale=w_scales[:, z, t * P : (t + 1) * P],
-                    rhs=x_codes[z, h][:, cols].bitcast(FP8X4),
-                    rhs_scale=x_scales[z, h][:, cols],
+                    rhs=codes.bitcast(FP8X4),
+                    rhs_scale=scales,
                     start=(z == 0 and t == 0),
                     stop=(z == PASSES - 1 and t == PACK - 1),
                 )
@@ -145,19 +142,27 @@ def tile_moe_soft_larger_of_two_experts_pl_kernel(
             picked[:].rearrange("p t (c i) -> p c t i", i=4),
         )
 
+        places = x_bf[1][:].rearrange("p (c j) t -> p c j t", j=CHUNK)
+
+        def gather_half(rows, h, t):
+            target = places[:, 1:3, :, t] if h == 0 else places[:, 0:4:3, :, t]
+            nc.vector.tensor_copy(target, rows[:].indirect(offsets[:, h * HALF // 16 : (h + 1) * HALF // 16]))
+
         for t in range(PACK - 1):
             rows = load_x(1, t)
-            nc.vector.tensor_copy(x_bf[1][:, :, t], rows[:].indirect(offsets[:]))
+            gather_half(rows, 0, t)
+            gather_half(rows, 1, t)
             if t == 0:
-                quantise_x(0, 0)
-        quantise_x(0, 1)
+                quantise_x(0, (0, 1), 0)
+                quantise_x(0, (2,), 2)
+        quantise_x(0, (3,), 3, tag=f"x_rows{PACK - 2}")
         rows = load_x(1, PACK - 1)
-        for h in range(2):
-            nc.vector.tensor_copy(
-                x_bf[1][:, h * HALF : (h + 1) * HALF, PACK - 1],
-                rows[:].indirect(offsets[:, h * HALF // 16 : (h + 1) * HALF // 16]),
-            )
-            quantise_x(1, h)
+        gather_half(rows, 0, PACK - 1)
+        quantise_x(1, (0,), 1)
+        quantise_x(1, (1,), 2)
+        gather_half(rows, 1, PACK - 1)
+        quantise_x(1, (2,), 0)
+        quantise_x(1, (3,), 3)
 
         y_codes = keep.tile([P, J], U32, name="y_codes", align_bytes=64)
         y_plane = keep.tile([P, J], U8, name="y_plane", align_bytes=64)
@@ -183,23 +188,26 @@ def tile_moe_soft_larger_of_two_experts_pl_kernel(
                 ALU.add,
             )
 
-        def weigh(c):
+        def weigh_on_gpsimd(c, slots):
             cols = slice(c * CHUNK, (c + 1) * CHUNK)
-            y[c] = work.tile([P, PACK, CHUNK], F32, name="y")
-            if c < 2:
-                nc.gpsimd.tensor_tensor(
-                    y[c][:], mix[c][:], gate[:, cols].unsqueeze(1).to_broadcast([P, PACK, CHUNK]), ALU.mult
-                )
-            else:
-                quarter = CHUNK // CHUNKS
-                gate_psum = acc_a[0][:].rearrange("q r p -> q p r")[:, c * quarter : (c + 1) * quarter, :]
-                nc.vector.tensor_tensor(
-                    y[c][:].rearrange("p t (a r) -> p t a r", r=CHUNKS),
-                    mix[c][:].rearrange("p t (a r) -> p t a r", r=CHUNKS),
-                    gate_psum.unsqueeze(1).to_broadcast([P, PACK, quarter, CHUNKS]),
-                    ALU.mult,
-                )
-            nc.sync.dma_start(y_rows[:, :, cols], y[c][:])
+            count = slots.stop - slots.start
+            nc.gpsimd.tensor_tensor(
+                y[c][:, slots, :],
+                mix[c][:, slots, :],
+                gate[:, cols].unsqueeze(1).to_broadcast([P, count, CHUNK]),
+                ALU.mult,
+            )
+
+        def weigh_on_vector(c, slots):
+            quarter = CHUNK // CHUNKS
+            count = slots.stop - slots.start
+            gate_psum = acc_a[0][:].rearrange("q r p -> q p r")[:, c * quarter : (c + 1) * quarter, :]
+            nc.vector.tensor_tensor(
+                y[c][:, slots, :].rearrange("p t (a r) -> p t a r", r=CHUNKS),
+                mix[c][:, slots, :].rearrange("p t (a r) -> p t a r", r=CHUNKS),
+                gate_psum.unsqueeze(1).to_broadcast([P, count, quarter, CHUNKS]),
+                ALU.mult,
+            )
 
         subtract(0)
         for r in range(CHUNKS):
@@ -210,25 +218,37 @@ def tile_moe_soft_larger_of_two_experts_pl_kernel(
         subtract(3)
         for c in range(1, CHUNKS):
             blend(c)
+        y_half = [keep.tile([P, PACK, HALF], F32, name=f"y_half{h}") for h in range(2)]
         for c in range(CHUNKS):
-            weigh(c)
-        for h in range(2):
-            y_bf = keep.tile([P, HALF, PACK], BF16, name=f"y_bf{h}", tag=f"diff{last - h}", align_bytes=64)
-            for i in range(2):
-                c = 2 * h + i
-                dst = y_bf[:, i * CHUNK : (i + 1) * CHUNK, :].rearrange("p (c i) t -> p c t i", i=4)
-                src = y[c][:].rearrange("p t (c i) -> p c t i", i=4)
-                if c < last:
-                    nc.scalar.copy(dst, src)
-                else:
-                    nc.vector.tensor_copy(dst, src)
-            cols = slice(h * HALF, (h + 1) * HALF)
+            y[c] = y_half[c // 2][:, :, c % 2 * CHUNK : (c % 2 + 1) * CHUNK]
+        weigh_on_gpsimd(0, slice(0, 4))
+        weigh_on_gpsimd(1, slice(0, 4))
+        weigh_on_gpsimd(2, slice(0, 2))
+        weigh_on_vector(3, slice(0, 4))
+        weigh_on_vector(2, slice(2, 4))
+        for c in (0, 1):
+            nc.sync.dma_start(y_rows[:, :, c * CHUNK : (c + 1) * CHUNK], y[c])
+        nc.sync.dma_start(y_rows[:, :, HALF:], y_half[1][:])
+        def round_and_quantise(chunks, copy, tag):
+            width = len(chunks) * CHUNK
+            y_bf = keep.tile([P, width, PACK], BF16, name=f"y_bf{chunks[0]}", tag=tag, align_bytes=64)
+            for i, c in enumerate(chunks):
+                copy(
+                    y_bf[:, i * CHUNK : (i + 1) * CHUNK, :].rearrange("p (c i) t -> p c t i", i=4),
+                    y[c].rearrange("p t (c i) -> p c t i", i=4),
+                )
+            cols = slice(chunks[0] * CHUNK, chunks[0] * CHUNK + width)
             nc.vector.quantize_mx(
                 out=y_codes[:, cols].bitcast(FP8X4),
                 scales=y_plane[:, cols],
                 in_=y_bf[:].rearrange("p j t -> p (j t)"),
             )
-            nc.sync.dma_start(y_words[:, cols], y_codes[:, cols].bitcast(I32))
+
+        round_and_quantise((0, 1), nc.scalar.copy, "diff3")
+        nc.sync.dma_start(y_words[:, :HALF], y_codes[:, :HALF].bitcast(I32))
+        round_and_quantise((3,), nc.scalar.copy, "diff2")
+        round_and_quantise((2,), nc.vector.tensor_copy, "diff3")
+        nc.sync.dma_start(y_words[:, HALF:], y_codes[:, HALF:].bitcast(I32))
         for r in range(4):
             queue = nc.sync if r % 2 == 0 else nc.scalar
             queue.dma_start(y_scales[r:16:4, :], y_plane[r:P:32, :].bitcast(I32))

@@ -47,8 +47,41 @@ def tile_moe_soft_larger_of_two_experts_pl_kernel(
         work = ctx.enter_context(tc.tile_pool(name="work", bufs=4))
         psum = ctx.enter_context(tc.psum_pool(name="psum", bufs=1))
 
+        x_tiles = {}
+
+        def load_x(index):
+            z, t = divmod(index, PACK)
+            x_tiles[z, t] = keep.tile([P, T], F32, name=f"x_rows{z}{t}", tag=f"x_rows{z}{t}", align_bytes=64)
+            nc.sync.dma_start(x_tiles[z, t][:], x_rows[z, t])
+
+        scale_rows = keep.tile([P, PASSES, N // 4], I32, name="scale_rows")
+
+        def load_scale_rows(first, stop):
+            for row in range(first, stop):
+                scales = wa_scales if row < B_ROW else wb_scales
+                nc.sync.dma_start(
+                    scale_rows[row:P:32],
+                    scales[:, row % 4 : 16 : 4, :].rearrange("z q c -> q z c").bitcast(I32),
+                )
+
         offsets = keep.tile([P, J // 16], U16, name="offsets")
+        raw_a = keep.tile([P, PASSES, 2 * N], U8, name="raw_a", align_bytes=64)
+        raw_b = keep.tile([P, PASSES, N], I32, name="raw_b", align_bytes=64)
+        gate_cols = keep.tile([P, CHUNKS], F32, name="gate_cols")
+        load_x(0)
         nc.sync.dma_start(offsets[:], offs)
+        load_scale_rows(0, 3)
+        nc.sync.dma_start(raw_a[:].bitcast(I32), wa_words.rearrange("z p c -> p z c").bitcast(I32))
+        nc.sync.dma_start(raw_b[:], wb_words.rearrange("z p n t -> p z (n t)").bitcast(I32))
+        load_x(1)
+        load_x(2)
+        load_scale_rows(3, 8)
+        load_x(3)
+        load_x(4)
+        load_x(5)
+        nc.sync.dma_start(gate_cols[:], ga.rearrange("o (p c) -> (o p) c", c=CHUNKS))
+        load_x(6)
+        load_x(7)
 
         raw_scales = keep.tile([P, PASSES, N], U8, name="raw_scales", align_bytes=64)
         nc.gpsimd.memset(raw_scales[:].bitcast(I32), 0)
@@ -56,26 +89,6 @@ def tile_moe_soft_larger_of_two_experts_pl_kernel(
         make_identity(nc, ident[:])
         warm = keep.tile([P, 1], F32, name="warm")
         nc.scalar.activation(warm[:], ident[:, 0:1], ACT.Silu)
-
-        def load_x(z, t):
-            rows = keep.tile([P, T], F32, name=f"x_rows{z}{t}", tag=f"x_rows{t}", align_bytes=64)
-            nc.sync.dma_start(rows[:], x_rows[z, t])
-            return rows
-
-        x_tiles = {(0, 0): load_x(0, 0)}
-
-        raw_a = keep.tile([P, PASSES, 2 * N], U8, name="raw_a", align_bytes=64)
-        nc.sync.dma_start(raw_a[:].bitcast(I32), wa_words.rearrange("z p c -> p z c").bitcast(I32))
-        raw_b = keep.tile([P, PASSES, N], I32, name="raw_b", align_bytes=64)
-        nc.sync.dma_start(raw_b[:], wb_words.rearrange("z p n t -> p z (n t)").bitcast(I32))
-        for first_row, scales in ((0, wa_scales), (B_ROW, wb_scales)):
-            for r in range(4):
-                nc.scalar.dma_start(
-                    raw_scales[first_row + r : P : 32].bitcast(I32),
-                    scales[:, r:16:4, :].rearrange("z q c -> q z c").bitcast(I32),
-                )
-        gate_cols = keep.tile([P, CHUNKS], F32, name="gate_cols")
-        nc.scalar.dma_start(gate_cols[:], ga.rearrange("o (p c) -> (o p) c", c=CHUNKS))
 
         acc_a = [psum.tile([P, PACK, CHUNK], F32, name=f"acc_a{c}") for c in range(CHUNKS)]
         acc_b = [psum.tile([P, PACK, CHUNK], F32, name=f"acc_b{c}") for c in range(CHUNKS)]
@@ -128,14 +141,14 @@ def tile_moe_soft_larger_of_two_experts_pl_kernel(
 
         picked = keep.tile([P, PACK, J], F32, name="picked")
         for t in range(PACK):
-            if t + 1 < PACK:
-                x_tiles[(0, t + 1)] = load_x(0, t + 1)
             nc.vector.tensor_copy(picked[:, t, :], x_tiles[(0, t)][:].indirect(offsets[:]))
             if t == 0:
                 deal_columns(nc, a_words[:].bitcast(U16), raw_a[:].bitcast(U16), 8)
             if t == 1:
                 deal_columns(nc, b_words[:], raw_b[:], 4)
             if t == 2:
+                for q in range(0, P, 32):
+                    nc.vector.tensor_copy(raw_scales[q : q + 8].bitcast(I32), scale_rows[q : q + 8])
                 deal_columns(nc, w_scales[:], raw_scales[:], 16)
         nc.scalar.copy(
             x_bf[0][:].rearrange("p (c i) t -> p c t i", i=4),
@@ -149,14 +162,14 @@ def tile_moe_soft_larger_of_two_experts_pl_kernel(
             nc.vector.tensor_copy(target, rows[:].indirect(offsets[:, h * HALF // 16 : (h + 1) * HALF // 16]))
 
         for t in range(PACK - 1):
-            rows = load_x(1, t)
+            rows = x_tiles[1, t]
             gather_half(rows, 0, t)
             gather_half(rows, 1, t)
             if t == 0:
                 quantise_x(0, (0, 1), 0)
                 quantise_x(0, (2,), 2)
-        quantise_x(0, (3,), 3, tag=f"x_rows{PACK - 2}")
-        rows = load_x(1, PACK - 1)
+        quantise_x(0, (3,), 3, tag=f"x_rows1{PACK - 2}")
+        rows = x_tiles[1, PACK - 1]
         gather_half(rows, 0, PACK - 1)
         quantise_x(1, (0,), 1)
         quantise_x(1, (1,), 2)

from contextlib import ExitStack

import concourse.mybir as mybir
from concourse.masks import make_identity

K, T, J, N = 1024, 2048, 512, 512
FLOPS = 2 * 2 * K * N * J

F32 = mybir.dt.float32
BF16 = mybir.dt.bfloat16
I32 = mybir.dt.int32
U32 = mybir.dt.uint32
U16 = mybir.dt.uint16
U8 = mybir.dt.uint8
FP8X4 = mybir.dt.float8_e4m3fn_x4
FP4X4 = mybir.dt.float4_e2m1fn_x4
ALU = mybir.AluOpType
ACT = mybir.ActivationFunctionType

P = 128
PACK = 4
PASSES = K // (P * PACK)
CHUNK = 128
CHUNKS = J // CHUNK
HALF = J // 2
B_ROW = 4


def deal_columns(nc, dealt, raw, run):
    nc.vector.tensor_copy(
        out=dealt.rearrange("p z (t c i) -> p z c t i", t=PACK, i=run),
        in_=raw.rearrange("p z (c i t) -> p z c t i", t=PACK, i=run),
    )


def tile_moe_soft_larger_of_two_experts_pl_kernel(
    tc, xt, wa_words, wa_scales, wb_words, wb_scales, ga, offs, out_0, out_1, out_2
):
    nc = tc.nc
    x_rows = xt.rearrange("(z p t) c -> z t p c", p=P, t=PACK)
    y_rows = out_0.rearrange("(p t) j -> p t j", t=PACK)
    y_words = out_1[0].rearrange("p j t -> p (j t)").bitcast(I32)
    y_scales = out_2[0].bitcast(I32)

    with ExitStack() as ctx:
        keep = ctx.enter_context(tc.tile_pool(name="keep", bufs=1))
        work = ctx.enter_context(tc.tile_pool(name="work", bufs=4))
        psum = ctx.enter_context(tc.psum_pool(name="psum", bufs=1))

        x_tiles = {}

        def load_x(index):
            z, t = divmod(index, PACK)
            x_tiles[z, t] = keep.tile([P, T], F32, name=f"x_rows{z}{t}", tag=f"x_rows{z}{t}", align_bytes=64)
            nc.sync.dma_start(x_tiles[z, t][:], x_rows[z, t])

        scale_rows = keep.tile([P, PASSES, N // 4], I32, name="scale_rows")

        def load_scale_rows(first, stop):
            for row in range(first, stop):
                scales = wa_scales if row < B_ROW else wb_scales
                nc.sync.dma_start(
                    scale_rows[row:P:32],
                    scales[:, row % 4 : 16 : 4, :].rearrange("z q c -> q z c").bitcast(I32),
                )

        offsets = keep.tile([P, J // 16], U16, name="offsets")
        raw_a = keep.tile([P, PASSES, 2 * N], U8, name="raw_a", align_bytes=64)
        raw_b = keep.tile([P, PASSES, N], I32, name="raw_b", align_bytes=64)
        gate_cols = keep.tile([P, CHUNKS], F32, name="gate_cols")
        load_x(0)
        nc.sync.dma_start(offsets[:], offs)
        load_scale_rows(0, 3)
        nc.sync.dma_start(raw_a[:].bitcast(I32), wa_words.rearrange("z p c -> p z c").bitcast(I32))
        nc.sync.dma_start(raw_b[:], wb_words.rearrange("z p n t -> p z (n t)").bitcast(I32))
        load_x(1)
        load_x(2)
        load_scale_rows(3, 8)
        load_x(3)
        load_x(4)
        load_x(5)
        nc.sync.dma_start(gate_cols[:], ga.rearrange("o (p c) -> (o p) c", c=CHUNKS))
        load_x(6)
        load_x(7)

        raw_scales = keep.tile([P, PASSES, N], U8, name="raw_scales", align_bytes=64)
        nc.gpsimd.memset(raw_scales[:].bitcast(I32), 0)
        ident = keep.tile([P, P], F32, name="ident")
        make_identity(nc, ident[:])
        warm = keep.tile([P, 1], F32, name="warm")
        nc.scalar.activation(warm[:], ident[:, 0:1], ACT.Silu)

        acc_a = [psum.tile([P, PACK, CHUNK], F32, name=f"acc_a{c}") for c in range(CHUNKS)]
        acc_b = [psum.tile([P, PACK, CHUNK], F32, name=f"acc_b{c}") for c in range(CHUNKS)]

        gate = keep.tile([P, J], F32, name="gate")
        for c in range(CHUNKS):
            nc.tensor.transpose(acc_a[-1][:, c, :], gate_cols[:, c : c + 1].to_broadcast([P, P]), ident[:])
        nc.scalar.copy(gate[:].rearrange("q (p c) -> q p c", c=CHUNKS), acc_a[-1][:].rearrange("q c p -> q p c"))

        a_words = keep.tile([P, PASSES, 2 * N], U8, name="a_words", align_bytes=64)
        b_words = keep.tile([P, PASSES, N], I32, name="b_words", align_bytes=64)
        w_scales = keep.tile([P, PASSES, N], U8, name="w_scales", align_bytes=64)

        x_bf = [keep.tile([P, J, PACK], BF16, name=f"x_bf{z}", align_bytes=64) for z in range(PASSES)]

        def quantise_x(z, chunks, place, tag=None):
            width = len(chunks) * CHUNK
            name = f"{z}{chunks[0]}"
            codes = keep.tile([P, width], U32, name=f"x_codes{name}", tag=tag or f"x_codes{name}", align_bytes=64)
            scales = keep.tile([P, width], U8, name=f"x_scales{name}", align_bytes=64)
            nc.vector.quantize_mx(
                out=codes[:].bitcast(FP8X4),
                scales=scales[:],
                in_=x_bf[z][:, place * CHUNK : place * CHUNK + width, :].rearrange("p j t -> p (j t)"),
            )
            for i, c in enumerate(chunks):
                multiply(z, c, codes[:, i * CHUNK : (i + 1) * CHUNK], scales[:, i * CHUNK : (i + 1) * CHUNK])

        def multiply(z, c, codes, scales):
            for t in range(PACK):
                nc.tensor.matmul_mx(
                    out=acc_b[c][:, t, :],
                    lhsT=b_words[:, z, t * P : (t + 1) * P].bitcast(FP8X4),
                    lhsT_scale=w_scales[B_ROW:P, z, t * P : (t + 1) * P],
                    rhs=codes.bitcast(FP8X4),
                    rhs_scale=scales,
                    start=(z == 0 and t == 0),
                    stop=(z == PASSES - 1 and t == PACK - 1),
                )
            for t in range(PACK):
                nc.tensor.matmul_mx(
                    out=acc_a[c][:, t, :],
                    lhsT=a_words[:, z, 2 * t * P : 2 * (t + 1) * P].bitcast(FP4X4),
                    lhsT_scale=w_scales[:, z, t * P : (t + 1) * P],
                    rhs=codes.bitcast(FP8X4),
                    rhs_scale=scales,
                    start=(z == 0 and t == 0),
                    stop=(z == PASSES - 1 and t == PACK - 1),
                )

        picked = keep.tile([P, PACK, J], F32, name="picked")
        for t in range(PACK):
            nc.vector.tensor_copy(picked[:, t, :], x_tiles[(0, t)][:].indirect(offsets[:]))
            if t == 0:
                deal_columns(nc, a_words[:].bitcast(U16), raw_a[:].bitcast(U16), 8)
            if t == 1:
                deal_columns(nc, b_words[:], raw_b[:], 4)
            if t == 2:
                for q in range(0, P, 32):
                    nc.vector.tensor_copy(raw_scales[q : q + 8].bitcast(I32), scale_rows[q : q + 8])
                deal_columns(nc, w_scales[:], raw_scales[:], 16)
        nc.scalar.copy(
            x_bf[0][:].rearrange("p (c i) t -> p c t i", i=4),
            picked[:].rearrange("p t (c i) -> p c t i", i=4),
        )

        places = x_bf[1][:].rearrange("p (c j) t -> p c j t", j=CHUNK)

        def gather_half(rows, h, t):
            target = places[:, 1:3, :, t] if h == 0 else places[:, 0:4:3, :, t]
            nc.vector.tensor_copy(target, rows[:].indirect(offsets[:, h * HALF // 16 : (h + 1) * HALF // 16]))

        for t in range(PACK - 1):
            rows = x_tiles[1, t]
            gather_half(rows, 0, t)
            gather_half(rows, 1, t)
            if t == 0:
                quantise_x(0, (0, 1), 0)
                quantise_x(0, (2,), 2)
        quantise_x(0, (3,), 3, tag=f"x_rows1{PACK - 2}")
        rows = x_tiles[1, PACK - 1]
        gather_half(rows, 0, PACK - 1)
        quantise_x(1, (0,), 1)
        quantise_x(1, (1,), 2)
        gather_half(rows, 1, PACK - 1)
        quantise_x(1, (2,), 0)
        quantise_x(1, (3,), 3)

        y_codes = keep.tile([P, J], U32, name="y_codes", align_bytes=64)
        y_plane = keep.tile([P, J], U8, name="y_plane", align_bytes=64)
        last = CHUNKS - 1
        diff, soft, mix, y = {}, {}, {}, {}

        def subtract(c):
            b_sb = work.tile([P, PACK, CHUNK], F32, name="b_sb")
            nc.scalar.copy(b_sb[:], acc_b[c][:])
            diff[c] = keep.tile([P, PACK, CHUNK], F32, name=f"diff{c}", tag=f"diff{c}", align_bytes=64)
            nc.vector.tensor_tensor(diff[c][:], acc_a[c][:], b_sb[:], ALU.subtract)

        def blend(c):
            soft = work.tile([P, PACK, CHUNK], F32, name="soft")
            nc.scalar.activation(soft[:], diff[c][:], ACT.Silu, scale=0.5)
            mix[c] = work.tile([P, PACK, CHUNK], F32, name="mix")
            nc.vector.scalar_tensor_tensor(
                mix[c][:].rearrange("p t j -> p (t j)"),
                soft[:].rearrange("p t j -> p (t j)"),
                2.0,
                acc_b[c][:].rearrange("p t j -> p (t j)"),
                ALU.mult,
                ALU.add,
            )

        def weigh_on_gpsimd(c, slots):
            cols = slice(c * CHUNK, (c + 1) * CHUNK)
            count = slots.stop - slots.start
            nc.gpsimd.tensor_tensor(
                y[c][:, slots, :],
                mix[c][:, slots, :],
                gate[:, cols].unsqueeze(1).to_broadcast([P, count, CHUNK]),
                ALU.mult,
            )

        def weigh_on_vector(c, slots):
            quarter = CHUNK // CHUNKS
            count = slots.stop - slots.start
            gate_psum = acc_a[0][:].rearrange("q r p -> q p r")[:, c * quarter : (c + 1) * quarter, :]
            nc.vector.tensor_tensor(
                y[c][:, slots, :].rearrange("p t (a r) -> p t a r", r=CHUNKS),
                mix[c][:, slots, :].rearrange("p t (a r) -> p t a r", r=CHUNKS),
                gate_psum.unsqueeze(1).to_broadcast([P, count, quarter, CHUNKS]),
                ALU.mult,
            )

        subtract(0)
        for r in range(CHUNKS):
            nc.tensor.transpose(acc_a[0][:, r, :], gate_cols[:, r : r + 1].to_broadcast([P, P]), ident[:])
        subtract(1)
        subtract(2)
        blend(0)
        subtract(3)
        for c in range(1, CHUNKS):
            blend(c)
        y_half = [keep.tile([P, PACK, HALF], F32, name=f"y_half{h}") for h in range(2)]
        for c in range(CHUNKS):
            y[c] = y_half[c // 2][:, :, c % 2 * CHUNK : (c % 2 + 1) * CHUNK]
        weigh_on_gpsimd(0, slice(0, 4))
        weigh_on_gpsimd(1, slice(0, 4))
        weigh_on_gpsimd(2, slice(0, 2))
        weigh_on_vector(3, slice(0, 4))
        weigh_on_vector(2, slice(2, 4))
        for c in (0, 1):
            nc.sync.dma_start(y_rows[:, :, c * CHUNK : (c + 1) * CHUNK], y[c])
        nc.sync.dma_start(y_rows[:, :, HALF:], y_half[1][:])
        def round_and_quantise(chunks, copy, tag):
            width = len(chunks) * CHUNK
            y_bf = keep.tile([P, width, PACK], BF16, name=f"y_bf{chunks[0]}", tag=tag, align_bytes=64)
            for i, c in enumerate(chunks):
                copy(
                    y_bf[:, i * CHUNK : (i + 1) * CHUNK, :].rearrange("p (c i) t -> p c t i", i=4),
                    y[c].rearrange("p t (c i) -> p c t i", i=4),
                )
            cols = slice(chunks[0] * CHUNK, chunks[0] * CHUNK + width)
            nc.vector.quantize_mx(
                out=y_codes[:, cols].bitcast(FP8X4),
                scales=y_plane[:, cols],
                in_=y_bf[:].rearrange("p j t -> p (j t)"),
            )

        round_and_quantise((0, 1), nc.scalar.copy, "diff3")
        nc.sync.dma_start(y_words[:, :HALF], y_codes[:, :HALF].bitcast(I32))
        round_and_quantise((3,), nc.scalar.copy, "diff2")
        round_and_quantise((2,), nc.vector.tensor_copy, "diff3")
        nc.sync.dma_start(y_words[:, HALF:], y_codes[:, HALF:].bitcast(I32))
        for r in range(4):
            queue = nc.sync if r % 2 == 0 else nc.scalar
            queue.dma_start(y_scales[r:16:4, :], y_plane[r:P:32, :].bitcast(I32))
